import numpy as np
import ml_dtypes


def mxq(x, axis, fmt="e4m3"):
    dtype, down = {"e4m3": (ml_dtypes.float8_e4m3fn, 7), "e5m2": (ml_dtypes.float8_e5m2, 14)}[fmt]
    v = np.moveaxis(np.asarray(x, np.float32).astype(ml_dtypes.bfloat16).astype(np.float64), axis, -1)
    blocks = v.reshape(v.shape[:-1] + (-1, 32))
    amax = np.abs(blocks).max(-1, keepdims=True)
    byte = np.maximum(np.where(amax > 0, np.frexp(amax)[1] - 1 + 127, 0) - down, 1)
    scale = np.exp2(byte - 127.0)
    codes = (blocks / scale).astype(np.float32).astype(dtype).astype(np.float64)
    return np.moveaxis((codes * scale).reshape(v.shape), -1, axis)


WIDE = False


def mx_kscale(k):
    if not WIDE:
        return np.ones(k)
    levels = np.array([10, -10, 5, -5, 0])
    if k % 512:
        return np.exp2(np.random.permutation(np.resize(levels, k // 32))).repeat(32)
    a = np.empty((k // 512, 16))
    for p in range(k // 512):
        a[p, :8] = np.random.permutation(np.resize(levels, 8))
        for g in range(8):
            far = levels[np.abs(levels - a[p, g]) >= 10]
            a[p, g + 8] = far[np.random.randint(len(far))]
    return np.exp2(a.ravel()).repeat(32)


def f64(x):
    return np.asarray(x).astype(np.float64)


def striped(idx):
    return np.tile(np.asarray(idx).reshape(-1, 16).T, (8, 1)).astype(np.uint16)


def unstriped(offs):
    return offs[:16].T.reshape(-1).astype(np.int64)


E2M1 = np.array([0.0, 0.5, 1.0, 1.5, 2.0, 3.0, 4.0, 6.0, -0.0, -0.5, -1.0, -1.5, -2.0, -3.0, -4.0, -6.0])


def pack_weight(w, fmt):
    k, n = w.shape
    w = f64(np.asarray(w, np.float32).astype(ml_dtypes.bfloat16)).reshape(k // 32, 32, n)
    amax = np.abs(w).max(1)
    if fmt == "e4m3":
        byte = np.frexp(amax)[1] - 1 + 127 - 7
    else:
        mant, ex = np.frexp(amax / 6.0)
        byte = np.where(mant > 0.5, ex, ex - 1) + 127
    byte = np.clip(np.where(amax > 0, byte, 1), 1, 254)
    scaled = (w * np.exp2(127.0 - byte)[:, None, :]).reshape(k, n).astype(np.float32)
    by_word = np.ascontiguousarray(scaled.reshape(k // 512, 128, 4, n).transpose(0, 1, 3, 2))
    if fmt == "e4m3":
        words = by_word.astype(ml_dtypes.float8_e4m3fn).view(np.uint8)
    else:
        c = by_word.astype(ml_dtypes.float4_e2m1fn).view(np.uint8) & 0xF
        words = (c[..., 0::2] | (c[..., 1::2] << 4)).reshape(k // 512, 128, 2 * n)
    return np.ascontiguousarray(words), np.ascontiguousarray(byte.astype(np.uint8).reshape(k // 512, 16, n))


def unpack_weight(words, scales, fmt):
    g, _, n = scales.shape
    words = np.ascontiguousarray(words).reshape(g, 128, n, -1)
    if fmt == "e4m3":
        vals = words.view(ml_dtypes.float8_e4m3fn).astype(np.float64)
    else:
        nib = np.empty((g, 128, n, 4), np.uint8)
        nib[..., 0::2] = words & 0xF
        nib[..., 1::2] = words >> 4
        vals = E2M1[nib]
    vals = vals * np.repeat(np.exp2(scales.astype(np.float64) - 127.0), 8, axis=1)[..., None]
    return vals.transpose(0, 1, 3, 2).reshape(g * 512, n)


D, T, U, I, J, G = 512, 1024, 1024, 256, 512, 64


def setup_inputs():
    n = np.random.standard_normal
    idx = np.random.permutation(T)[:I]
    idx2 = np.random.permutation(U)[:J]
    fd = mx_kscale(D)
    tabbp = pack_weight(n((D, U)) / fd[:, None], "e2m1")
    return {
        "taba": (n((D, T)) * 1 / np.sqrt(D) * fd[:, None]).astype(np.float32),
        "dtab": (n((D, T)) * 1.3 / np.sqrt(D) * fd[:, None]).astype(np.float32),
        "tabb_words": tabbp[0],
        "tabb_scales": tabbp[1],
        "val": (np.random.uniform(-1.5, 1.5, (1, J))).astype(np.float32),
        "aim": (n((I, G)) * 1.0).astype(np.float32),
        "base": (0.3 * n((I, J))).astype(np.float32),
        "offs": striped(idx),
        "offs2": striped(idx2),
    }


def reference(taba, dtab, tabb_words, tabb_scales, val, aim, base, offs, offs2):
    idx = unstriped(offs)
    idx2 = unstriped(offs2)
    tabbu = unpack_weight(tabb_words, tabb_scales, "e2m1")
    tabaidxq = mxq(f64(taba)[:, idx], 0, "e4m3")
    tabbidx2g = tabbu[:, idx2]
    s = tabaidxq.T @ tabbidx2g
    dtabidxq = mxq(f64(dtab)[:, idx], 0, "e4m3")
    ts = dtabidxq.T @ tabbidx2g
    p = np.exp(s)
    z = p.reshape(I, G, J // G).sum(axis=2)
    ev = (p * f64(val)).reshape(I, G, J // G).sum(axis=2) / z
    dev = (ev - f64(aim)) * 2.0
    e1 = dev / z
    r1 = np.repeat(e1, J // G, axis=1)
    dz = dev * (p * f64(val)).reshape(I, G, J // G).sum(axis=2) / np.square(z) * (-1.0)
    r2 = np.repeat(dz, J // G, axis=1)
    dp = r1 * f64(val) + r2
    xp = ts * p
    xz = xp.reshape(I, G, J // G).sum(axis=2)
    xev = ((xp * f64(val)).reshape(I, G, J // G).sum(axis=2) - xz * (p * f64(val)).reshape(I, G, J // G).sum(axis=2) / z) / z
    xdev = xev * 2.0
    xe1 = (xdev - xz * dev / z) / z
    xr1 = np.repeat(xe1, J // G, axis=1)
    xdz = (xdev * (p * f64(val)).reshape(I, G, J // G).sum(axis=2) + (xp * f64(val)).reshape(I, G, J // G).sum(axis=2) * dev - xz * z * 2.0 * dev * (p * f64(val)).reshape(I, G, J // G).sum(axis=2) / np.square(z)) / np.square(z) * (-1.0)
    xr2 = np.repeat(xdz, J // G, axis=1)
    xdp = xr1 * f64(val) + xr2
    xds = xdp * p + xp * dp
    y = xds * 4.0 + f64(base)
    return y

@@ -1,0 +1,202 @@
+from contextlib import ExitStack
+
+import concourse.mybir as mybir
+from concourse.masks import make_identity
+
+D, T, U, I, J, G = 512, 1024, 1024, 256, 512, 64
+FLOPS = 2 * 2 * D * I * J
+
+F32 = mybir.dt.float32
+BF16 = mybir.dt.bfloat16
+I32 = mybir.dt.int32
+U32 = mybir.dt.uint32
+U16 = mybir.dt.uint16
+U8 = mybir.dt.uint8
+FP8X4 = mybir.dt.float8_e4m3fn_x4
+FP4X4 = mybir.dt.float4_e2m1fn_x4
+ALU = mybir.AluOpType
+ACT = mybir.ActivationFunctionType
+AX = mybir.AxisListType
+
+P = 128
+PACK = 4
+HALVES = I // P
+K = J // P
+
+
+def tile_attend_hvexpectedvalue_kernel(tc, taba, dtab, tabb_words, tabb_scales, val, aim, base, offs, offs2, out):
+    nc = tc.nc
+    with ExitStack() as ctx:
+        lists = ctx.enter_context(tc.tile_pool(name="lists", bufs=1))
+        sb = ctx.enter_context(tc.tile_pool(name="sb", bufs=1))
+        ps = ctx.enter_context(tc.psum_pool(name="ps", bufs=1))
+
+        offs2_sb = lists.tile([P, J // 16], U16, name="offs2_sb")
+        offs_sb = lists.tile([P, I // 16], U16, name="offs_sb")
+        words = sb.tile([P, U], U16, name="words", align_bytes=64)
+        scales = sb.tile([P, U], U8, name="scales", align_bytes=64)
+        nc.vector.memset(scales[:].bitcast(I32), 0)
+        nc.sync.dma_start(offs2_sb[:], offs2)
+        nc.sync.dma_start(words[:].bitcast(I32), tabb_words[0].bitcast(I32))
+        for q in range(4):
+            nc.scalar.dma_start(scales[32 * q : 32 * q + 4, :].bitcast(I32), tabb_scales[0, 4 * q : 4 * q + 4, :].bitcast(I32))
+        nc.sync.dma_start(offs_sb[:], offs)
+
+        def load_planes(table, name):
+            rows = table.rearrange("(p t) c -> p t c", t=PACK)
+            planes = []
+            for t in range(PACK):
+                plane = sb.tile([P, T], F32, name=f"{name}{t}")
+                nc.sync.dma_start(plane[:], rows[:, t, :])
+                planes.append(plane)
+            return planes
+
+        a_planes = load_planes(taba, "ta")
+        val_sb = sb.tile([P, K], F32, name="val_sb")
+        nc.sync.dma_start(val_sb[:], val.rearrange("o (p k) -> (o p) k", k=K))
+        aim_sb = sb.tile([P, HALVES, G], F32, name="aim_sb")
+        nc.sync.dma_start(aim_sb[:], aim.rearrange("(h p) g -> p h g", p=P))
+        d_planes = load_planes(dtab, "td")
+        base_sb = []
+        for h in range(HALVES):
+            b = sb.tile([P, J], F32, name=f"base{h}")
+            nc.sync.dma_start(b[:], base[h * P : (h + 1) * P, :])
+            base_sb.append(b)
+
+        ident = sb.tile([P, P], F32, name="ident")
+        make_identity(nc, ident[:])
+
+        got_words = sb.tile([P, J], U16, name="got_words", align_bytes=64)
+        got_scales = sb.tile([P, J], U8, name="got_scales", align_bytes=64)
+        b_words = sb.tile([P, K, P], U16, name="b_words", align_bytes=64)
+        b_scales = sb.tile([P, K, P], U8, name="b_scales", align_bytes=64)
+        nc.vector.tensor_copy(got_words[:], words[:].indirect(offs2_sb[:]))
+        nc.vector.tensor_copy(got_scales[:], scales[:].indirect(offs2_sb[:]))
+        nc.vector.tensor_copy(b_words[:], got_words[:].rearrange("p (c k) -> p k c", k=K))
+        nc.vector.tensor_copy(b_scales[:], got_scales[:].rearrange("p (c k) -> p k c", k=K))
+
+        def gather_vector(picked, planes, t):
+            nc.vector.tensor_copy(picked[:, :, t], planes[t][:].indirect(offs_sb[:]))
+
+        def gather_scalar(picked, planes, t):
+            rounded = sb.tile([P, T], BF16, name=f"rounded{t}")
+            nc.scalar.activation(rounded[:], planes[t][:], ACT.Copy)
+            nc.scalar.activation(picked[:, :, t], rounded[:].indirect(offs_sb[:]), ACT.Copy)
+
+        def quantise(picked, name):
+            codes = sb.tile([P, I], U32, name=f"{name}_codes", align_bytes=64)
+            bytes8 = sb.tile([P, I], U8, name=f"{name}_scales", align_bytes=64)
+            nc.vector.quantize_mx(out=codes[:].bitcast(FP8X4), scales=bytes8[:], in_=picked[:].rearrange("p i t -> p (i t)"))
+            return codes, bytes8
+
+        def scores(codes, bytes8, h, tag):
+            bank = ps.tile([P, K, P], F32, name=f"{tag}{h}", tag=f"{tag}{h}")
+            cols = slice(h * P, (h + 1) * P)
+            for k in range(K):
+                nc.tensor.matmul_mx(out=bank[:, k, :], lhsT=b_words[:, k, :].bitcast(FP4X4), lhsT_scale=b_scales[:, k, :],
+                                    rhs=codes[:, cols].bitcast(FP8X4), rhs_scale=bytes8[:, cols], start=True, stop=True)
+            return bank
+
+        def turn_and_add(steps):
+            for n, (dst, src) in enumerate(steps):
+                nc.tensor.matmul(dst, src, ident[:], start=(n == 0), stop=(n == len(steps) - 1), is_transpose=True)
+
+        def times_val(pair):
+            for k in range(K):
+                nc.scalar.activation(pair[:, 0, k, :], pair[:, 1, k, :], ACT.Copy, scale=val_sb[:, k : k + 1])
+
+        def group_sums(pair, h, name):
+            bank = ps.tile([P, 2, P], F32, name=f"sum_{name}{h}", tag=f"sum{h}")
+            turn_and_add([(bank[:, q, :], pair[:, q, k, :]) for q in (1, 0) for k in range(K)])
+            sums = sb.tile([P, 2, G], F32, name=f"sums_{name}{h}")
+            nc.vector.tensor_reduce(sums[:], bank[:].rearrange("p q (g r) -> p q g r", r=2), AX.X, ALU.add)
+            return sums
+
+        def twice(ap):
+            return ap.unsqueeze(2).to_broadcast([P, G, 2])
+
+        a_picked = sb.tile([P, I, PACK], BF16, name="a_picked", align_bytes=64)
+        d_picked = sb.tile([P, I, PACK], BF16, name="d_picked", align_bytes=64)
+        for t in (0, 1):
+            gather_scalar(a_picked, a_planes, t)
+        for t in (2, 3):
+            gather_vector(a_picked, a_planes, t)
+        a_codes, a_scales = quantise(a_picked, "a")
+        s_bank = [scores(a_codes, a_scales, h, "s") for h in range(HALVES)]
+        pp = []
+        for h in range(HALVES):
+            pair = sb.tile([P, 2, K, P], F32, name=f"pp{h}")
+            nc.scalar.activation(pair[:, 1], s_bank[h][:], ACT.Exp)
+            times_val(pair)
+            pp.append(pair)
+        for t in range(PACK):
+            gather_vector(d_picked, d_planes, t)
+        d_codes, d_scales = quantise(d_picked, "d")
+        ts_bank = [scores(d_codes, d_scales, h, "t") for h in range(HALVES)]
+
+        coef = sb.tile([P, HALVES, 4, G], F32, name="coef")
+        fwd = sb.tile([P, HALVES, 2, G, 2], F32, name="fwd")
+        xx = []
+        for h in range(HALVES):
+            rz = coef[:, h, 0, :]
+            sums = group_sums(pp[h], h, "p")
+            nc.vector.reciprocal(rz, sums[:, 1, :])
+            pair = sb.tile([P, 2, K, P], F32, name=f"xx{h}")
+            nc.vector.tensor_tensor(pair[:, 1], ts_bank[h][:], pp[h][:, 1], ALU.mult)
+            times_val(pair)
+            xx.append(pair)
+            nc.vector.tensor_tensor(fwd[:, h, 0], twice(sums[:, 0, :]), twice(rz), ALU.mult)
+            dif = sb.tile([P, G], F32, name=f"dif{h}")
+            nc.vector.tensor_tensor(dif[:], aim_sb[:, h, :], fwd[:, h, 0, :, 0], ALU.subtract)
+            nc.vector.tensor_tensor(fwd[:, h, 1], twice(dif[:]), twice(rz), ALU.mult)
+
+        ev = fwd[:, :, 0, :, 0]
+        cc = fwd[:, :, 1, :, 0]
+        tmp = sb.tile([P, HALVES, G], F32, name="tmp")
+        tmp2 = sb.tile([P, HALVES, G], F32, name="tmp2")
+        nc.vector.tensor_tensor(tmp[:], coef[:, :, 0, :], ev, ALU.mult)
+        nc.vector.tensor_tensor(coef[:, :, 1:3, :], cc.unsqueeze(2).to_broadcast([P, HALVES, 2, G]),
+                                tmp[:].unsqueeze(2).to_broadcast([P, HALVES, 2, G]), ALU.subtract)
+        nc.vector.tensor_tensor(tmp2[:], cc, coef[:, :, 1, :], ALU.add)
+        nc.vector.scalar_tensor_tensor(coef[:, :, 3, :], tmp2[:], -1.0, ev, ALU.mult, ALU.mult)
+
+        t2 = []
+        for h in range(HALVES):
+            back = ps.tile([P, 2, P], F32, name=f"back_f{h}", tag=f"back{h}")
+            turn_and_add([(back[:, q, :], fwd[:, h, q].rearrange("p g r -> p (g r)")) for q in (1, 0)])
+            negc = sb.tile([P, P], F32, name=f"negc{h}")
+            nc.scalar.activation(negc[:], back[:, 1, :], ACT.Copy, scale=8.0)
+            slope = sb.tile([P, K, P], F32, name=f"slope{h}")
+            for k in range(K):
+                nc.vector.scalar_tensor_tensor(slope[:, k, :], back[:, 0, :], val_sb[:, k : k + 1], negc[:], ALU.subtract, ALU.mult)
+            t2.append(slope)
+
+        prods = []
+        terms = []
+        for h in range(HALVES):
+            sums = group_sums(xx[h], h, "x")
+            means = sb.tile([P, 2, G], F32, name=f"means{h}")
+            nc.vector.scalar_tensor_tensor(means[:], sums[:], 8.0, coef[:, h, 0, :].unsqueeze(1).to_broadcast([P, 2, G]), ALU.mult, ALU.mult)
+            prod = sb.tile([P, 2, 2 * G, 2], F32, name=f"prod{h}")
+            nc.vector.tensor_tensor(
+                prod[:],
+                coef[:, h].rearrange("p (a q) g -> p a (q g)", a=2).unsqueeze(3).to_broadcast([P, 2, 2 * G, 2]),
+                means[:].rearrange("p q g -> p (q g)").unsqueeze(1).unsqueeze(3).to_broadcast([P, 2, 2 * G, 2]),
+                ALU.mult)
+            prods.append(prod)
+        for h in range(HALVES):
+            three = sb.tile([P, 3, K, P], F32, name=f"terms{h}")
+            nc.vector.tensor_tensor(three[:, 2], xx[h][:, 1], t2[h][:], ALU.mult)
+            terms.append(three)
+        for h in range(HALVES):
+            back = ps.tile([P, 2, P], F32, name=f"back_x{h}", tag=f"back{h}")
+            flat = prods[h][:].rearrange("p a c r -> p a (c r)")
+            turn_and_add([(back[:, a, :], flat[:, a, q * P : (q + 1) * P]) for a in range(2) for q in range(2)])
+            for a in range(2):
+                nc.vector.tensor_tensor(terms[h][:, a], back[:, a, :].unsqueeze(1).to_broadcast([P, K, P]), pp[h][:, a], ALU.mult)
+        for h in range(HALVES):
+            total = ps.tile([P, K, P], F32, name=f"total{h}", tag=f"s{h}")
+            turn_and_add([(total[:, k, :], terms[h][:, a, k, :]) for a in (2, 0, 1) for k in range(K)])
+            res = sb.tile([P, P, K], F32, name=f"res{h}")
+            nc.vector.tensor_tensor(res[:], total[:].rearrange("i k p -> i p k"), base_sb[h][:].rearrange("i (p k) -> i p k", k=K), ALU.add)
+            nc.sync.dma_start(out[h * P : (h + 1) * P, :], res[:].rearrange("i p k -> i (p k)"))

@@ -22,6 +22,10 @@ P = 128
 PACK = 4
 HALVES = I // P
 K = J // P
+LIST_ROWS = 16
+HALF_LIST = P // LIST_ROWS
+K_STEP = 2
+MX_ALIGN = 64
 
 
 def tile_attend_hvexpectedvalue_kernel(tc, taba, dtab, tabb_words, tabb_scales, val, aim, base, offs, offs2, out):
@@ -31,19 +35,19 @@ def tile_attend_hvexpectedvalue_kernel(tc, taba, dtab, tabb_words, tabb_scales, 
         sb = ctx.enter_context(tc.tile_pool(name="sb", bufs=1))
         ps = ctx.enter_context(tc.psum_pool(name="ps", bufs=1))
 
-        offs2_sb = lists.tile([P, J // 16], U16, name="offs2_sb")
-        offs_sb = lists.tile([P, I // 16], U16, name="offs_sb")
-        words = sb.tile([P, U], U16, name="words", align_bytes=64)
-        scales = sb.tile([P, U], U8, name="scales", align_bytes=64)
-        nc.vector.memset(scales[:].bitcast(I32), 0)
+        offs2_sb = lists.tile([P, J // LIST_ROWS], U16, name="offs2_sb")
+        offs_sb = lists.tile([P, I // LIST_ROWS], U16, name="offs_sb")
+        words = sb.tile([P, U], U16, name="words", align_bytes=MX_ALIGN)
+        scales = sb.tile([P, U], U8, name="scales", align_bytes=MX_ALIGN)
+        nc.gpsimd.memset(scales[:].bitcast(I32), 0)
         nc.sync.dma_start(offs2_sb[:], offs2)
         nc.sync.dma_start(words[:].bitcast(I32), tabb_words[0].bitcast(I32))
         for q in range(4):
-            nc.scalar.dma_start(scales[32 * q : 32 * q + 4, :].bitcast(I32), tabb_scales[0, 4 * q : 4 * q + 4, :].bitcast(I32))
+            nc.sync.dma_start(scales[32 * q : 32 * q + 4, :].bitcast(I32), tabb_scales[0, 4 * q : 4 * q + 4, :].bitcast(I32))
         nc.sync.dma_start(offs_sb[:], offs)
 
         def load_planes(table, name):
-            rows = table.rearrange("(p t) c -> p t c", t=PACK)
+            rows = table.rearrange("(r t) c -> r t c", t=PACK)
             planes = []
             for t in range(PACK):
                 plane = sb.tile([P, T], F32, name=f"{name}{t}")
@@ -51,152 +55,172 @@ def tile_attend_hvexpectedvalue_kernel(tc, taba, dtab, tabb_words, tabb_scales, 
                 planes.append(plane)
             return planes
 
-        a_planes = load_planes(taba, "ta")
+        a_planes = load_planes(taba, "a_plane")
         val_sb = sb.tile([P, K], F32, name="val_sb")
-        nc.sync.dma_start(val_sb[:], val.rearrange("o (p k) -> (o p) k", k=K))
+        nc.sync.dma_start(val_sb[:], val.rearrange("o (r k) -> (o r) k", k=K))
+        d_planes = load_planes(dtab, "d_plane")
         aim_sb = sb.tile([P, HALVES, G], F32, name="aim_sb")
-        nc.sync.dma_start(aim_sb[:], aim.rearrange("(h p) g -> p h g", p=P))
-        d_planes = load_planes(dtab, "td")
+        nc.sync.dma_start(aim_sb[:], aim.rearrange("(h i) g -> i h g", i=P))
         base_sb = []
         for h in range(HALVES):
-            b = sb.tile([P, J], F32, name=f"base{h}")
-            nc.sync.dma_start(b[:], base[h * P : (h + 1) * P, :])
-            base_sb.append(b)
+            rows = sb.tile([P, J], F32, name=f"base{h}")
+            nc.sync.dma_start(rows[:], base[h * P : (h + 1) * P, :])
+            base_sb.append(rows)
 
         ident = sb.tile([P, P], F32, name="ident")
         make_identity(nc, ident[:])
 
-        got_words = sb.tile([P, J], U16, name="got_words", align_bytes=64)
-        got_scales = sb.tile([P, J], U8, name="got_scales", align_bytes=64)
-        b_words = sb.tile([P, K, P], U16, name="b_words", align_bytes=64)
-        b_scales = sb.tile([P, K, P], U8, name="b_scales", align_bytes=64)
-        nc.vector.tensor_copy(got_words[:], words[:].indirect(offs2_sb[:]))
+        got_words = sb.tile([P, J], U16, name="got_words", align_bytes=MX_ALIGN)
+        got_scales = sb.tile([P, J], U8, name="got_scales", align_bytes=MX_ALIGN)
+        b_words = sb.tile([P, K, P], U16, name="b_words", align_bytes=MX_ALIGN)
+        b_scales = sb.tile([P, K, P], U8, name="b_scales", align_bytes=MX_ALIGN)
         nc.vector.tensor_copy(got_scales[:], scales[:].indirect(offs2_sb[:]))
-        nc.vector.tensor_copy(b_words[:], got_words[:].rearrange("p (c k) -> p k c", k=K))
-        nc.vector.tensor_copy(b_scales[:], got_scales[:].rearrange("p (c k) -> p k c", k=K))
+        nc.vector.tensor_copy(got_words[:], words[:].indirect(offs2_sb[:]))
+        nc.vector.tensor_copy(b_words[:], got_words[:].rearrange("p (r k) -> p k r", k=K))
+        nc.vector.tensor_copy(b_scales[:], got_scales[:].rearrange("p (r k) -> p k r", k=K))
 
-        def gather_vector(picked, planes, t):
-            nc.vector.tensor_copy(picked[:, :, t], planes[t][:].indirect(offs_sb[:]))
+        def pieces(whole):
+            if whole:
+                return [(slice(0, I), slice(0, I // LIST_ROWS))]
+            return [(slice(h * P, (h + 1) * P), slice(h * HALF_LIST, (h + 1) * HALF_LIST)) for h in range(HALVES)]
 
-        def gather_scalar(picked, planes, t):
+        def gather_on_vector(picked, plane, t, whole):
+            for entries, columns in pieces(whole):
+                nc.vector.tensor_copy(picked[:, entries, t], plane[:].indirect(offs_sb[:, columns]))
+
+        def gather_on_scalar(picked, plane, t, whole):
             rounded = sb.tile([P, T], BF16, name=f"rounded{t}")
-            nc.scalar.activation(rounded[:], planes[t][:], ACT.Copy)
-            nc.scalar.activation(picked[:, :, t], rounded[:].indirect(offs_sb[:]), ACT.Copy)
+            nc.scalar.activation(rounded[:], plane[:], ACT.Copy)
+            for entries, columns in pieces(whole):
+                nc.scalar.activation(picked[:, entries, t], rounded[:].indirect(offs_sb[:, columns]), ACT.Copy)
 
-        def quantise(picked, name):
-            codes = sb.tile([P, I], U32, name=f"{name}_codes", align_bytes=64)
-            bytes8 = sb.tile([P, I], U8, name=f"{name}_scales", align_bytes=64)
-            nc.vector.quantize_mx(out=codes[:].bitcast(FP8X4), scales=bytes8[:], in_=picked[:].rearrange("p i t -> p (i t)"))
-            return codes, bytes8
-
-        def scores(codes, bytes8, h, tag):
-            bank = ps.tile([P, K, P], F32, name=f"{tag}{h}", tag=f"{tag}{h}")
-            cols = slice(h * P, (h + 1) * P)
+        def scores(picked, name, h):
+            codes = sb.tile([P, P], U32, name=f"{name}_codes{h}", align_bytes=MX_ALIGN)
+            code_scales = sb.tile([P, P], U8, name=f"{name}_scales{h}", align_bytes=MX_ALIGN)
+            nc.vector.quantize_mx(out=codes[:].bitcast(FP8X4), scales=code_scales[:],
+                                  in_=picked[:, h * P : (h + 1) * P, :].rearrange("p i t -> p (i t)"))
+            bank = ps.tile([P, K, P], F32, name=f"{name}_bank{h}")
             for k in range(K):
                 nc.tensor.matmul_mx(out=bank[:, k, :], lhsT=b_words[:, k, :].bitcast(FP4X4), lhsT_scale=b_scales[:, k, :],
-                                    rhs=codes[:, cols].bitcast(FP8X4), rhs_scale=bytes8[:, cols], start=True, stop=True)
+                                    rhs=codes[:].bitcast(FP8X4), rhs_scale=code_scales[:], start=True, stop=True)
             return bank
 
         def turn_and_add(steps):
-            for n, (dst, src) in enumerate(steps):
-                nc.tensor.matmul(dst, src, ident[:], start=(n == 0), stop=(n == len(steps) - 1), is_transpose=True)
+            for n, (place, tile) in enumerate(steps):
+                nc.tensor.matmul(place, tile, ident[:], start=(n == 0), stop=(n == len(steps) - 1), is_transpose=True)
 
         def times_val(pair):
             for k in range(K):
                 nc.scalar.activation(pair[:, 0, k, :], pair[:, 1, k, :], ACT.Copy, scale=val_sb[:, k : k + 1])
 
-        def group_sums(pair, h, name):
-            bank = ps.tile([P, 2, P], F32, name=f"sum_{name}{h}", tag=f"sum{h}")
-            turn_and_add([(bank[:, q, :], pair[:, q, k, :]) for q in (1, 0) for k in range(K)])
-            sums = sb.tile([P, 2, G], F32, name=f"sums_{name}{h}")
-            nc.vector.tensor_reduce(sums[:], bank[:].rearrange("p q (g r) -> p q g r", r=2), AX.X, ALU.add)
-            return sums
+        def group_sum(tiles, name, bank_tag, buffer_tag, align):
+            bank = ps.tile([P, P], F32, name=f"bank_{name}", tag=bank_tag)
+            turn_and_add([(bank[:], tiles[:, k, :]) for k in range(K)])
+            total = sb.tile([P, G], F32, name=name, tag=buffer_tag, align_bytes=align)
+            nc.vector.tensor_reduce(total[:], bank[:].rearrange("i (g e) -> i g e", e=2), AX.X, ALU.add)
+            return total
 
         def twice(ap):
-            return ap.unsqueeze(2).to_broadcast([P, G, 2])
+            return ap.unsqueeze(2).to_broadcast([P, ap.shape[1], 2])
 
-        a_picked = sb.tile([P, I, PACK], BF16, name="a_picked", align_bytes=64)
-        d_picked = sb.tile([P, I, PACK], BF16, name="d_picked", align_bytes=64)
+        a_picked = sb.tile([P, I, PACK], BF16, name="a_picked", align_bytes=MX_ALIGN)
+        d_picked = sb.tile([P, I, PACK], BF16, name="d_picked", align_bytes=MX_ALIGN)
         for t in (0, 1):
-            gather_scalar(a_picked, a_planes, t)
+            gather_on_scalar(a_picked, a_planes[t], t, whole=(t == 0))
         for t in (2, 3):
-            gather_vector(a_picked, a_planes, t)
-        a_codes, a_scales = quantise(a_picked, "a")
-        s_bank = [scores(a_codes, a_scales, h, "s") for h in range(HALVES)]
-        pp = []
+            gather_on_vector(a_picked, a_planes[t], t, whole=(t == 2))
+        s_banks = [scores(a_picked, "a", h) for h in range(HALVES)]
+        pv_p = []
         for h in range(HALVES):
-            pair = sb.tile([P, 2, K, P], F32, name=f"pp{h}")
-            nc.scalar.activation(pair[:, 1], s_bank[h][:], ACT.Exp)
-            times_val(pair)
-            pp.append(pair)
-        for t in range(PACK):
-            gather_vector(d_picked, d_planes, t)
-        d_codes, d_scales = quantise(d_picked, "d")
-        ts_bank = [scores(d_codes, d_scales, h, "t") for h in range(HALVES)]
+            pair = sb.tile([P, 2, K, P], F32, name=f"pv_p{h}")
+            nc.scalar.activation(pair[:, 1], s_banks[h][:], ACT.Exp)
+            pv_p.append(pair)
+        for h in range(HALVES):
+            times_val(pv_p[h])
 
-        coef = sb.tile([P, HALVES, 4, G], F32, name="coef")
-        fwd = sb.tile([P, HALVES, 2, G, 2], F32, name="fwd")
-        xx = []
+        turned = sb.tile([P, HALVES, 2, G, 2], F32, name="turned")
+        for t in range(PACK):
+            gather_on_vector(d_picked, d_planes[t], t, whole=(t < PACK - 1))
+        ts_banks = [scores(d_picked, "d", h) for h in range(HALVES)]
+
+        coef = sb.tile([P, HALVES, 4, G], F32, name="coef", tag="d_plane3")
+        xv_x = [sb.tile([P, 2, K, P], F32, name=f"xv_x{h}") for h in range(HALVES)]
+        for h in range(HALVES):
+            z = group_sum(pv_p[h][:, 1], f"z{h}", f"sum{h}", "d_plane2", None)
+            nc.vector.reciprocal(coef[:, h, 0, :], z[:])
+        gaps = []
         for h in range(HALVES):
             rz = coef[:, h, 0, :]
-            sums = group_sums(pp[h], h, "p")
-            nc.vector.reciprocal(rz, sums[:, 1, :])
-            pair = sb.tile([P, 2, K, P], F32, name=f"xx{h}")
-            nc.vector.tensor_tensor(pair[:, 1], ts_bank[h][:], pp[h][:, 1], ALU.mult)
-            times_val(pair)
-            xx.append(pair)
-            nc.vector.tensor_tensor(fwd[:, h, 0], twice(sums[:, 0, :]), twice(rz), ALU.mult)
-            dif = sb.tile([P, G], F32, name=f"dif{h}")
-            nc.vector.tensor_tensor(dif[:], aim_sb[:, h, :], fwd[:, h, 0, :, 0], ALU.subtract)
-            nc.vector.tensor_tensor(fwd[:, h, 1], twice(dif[:]), twice(rz), ALU.mult)
-
-        ev = fwd[:, :, 0, :, 0]
-        cc = fwd[:, :, 1, :, 0]
-        tmp = sb.tile([P, HALVES, G], F32, name="tmp")
-        tmp2 = sb.tile([P, HALVES, G], F32, name="tmp2")
-        nc.vector.tensor_tensor(tmp[:], coef[:, :, 0, :], ev, ALU.mult)
-        nc.vector.tensor_tensor(coef[:, :, 1:3, :], cc.unsqueeze(2).to_broadcast([P, HALVES, 2, G]),
-                                tmp[:].unsqueeze(2).to_broadcast([P, HALVES, 2, G]), ALU.subtract)
-        nc.vector.tensor_tensor(tmp2[:], cc, coef[:, :, 1, :], ALU.add)
-        nc.vector.scalar_tensor_tensor(coef[:, :, 3, :], tmp2[:], -1.0, ev, ALU.mult, ALU.mult)
-
-        t2 = []
-        for h in range(HALVES):
-            back = ps.tile([P, 2, P], F32, name=f"back_f{h}", tag=f"back{h}")
-            turn_and_add([(back[:, q, :], fwd[:, h, q].rearrange("p g r -> p (g r)")) for q in (1, 0)])
-            negc = sb.tile([P, P], F32, name=f"negc{h}")
-            nc.scalar.activation(negc[:], back[:, 1, :], ACT.Copy, scale=8.0)
-            slope = sb.tile([P, K, P], F32, name=f"slope{h}")
+            buffer_tag, align = (("d_picked", MX_ALIGN), ("d_plane2", None))[h]
+            w = group_sum(pv_p[h][:, 0], f"w{h}", f"back{h}", buffer_tag, align)
+            nc.vector.tensor_tensor(turned[:, h, 0], twice(w[:]), twice(rz), ALU.mult)
+            miss = sb.tile([P, G], F32, name=f"miss{h}")
+            nc.vector.tensor_tensor(miss[:], aim_sb[:, h, :], turned[:, h, 0, :, 0], ALU.subtract)
+            nc.vector.tensor_tensor(turned[:, h, 1], twice(miss[:]), twice(rz), ALU.mult)
+            ev_c = ps.tile([P, 2, P], F32, name=f"ev_c{h}", tag=f"a_bank{h}")
+            turn_and_add([(ev_c[:, n, :], turned[:, h, n].rearrange("i g e -> i (g e)")) for n in range(2)])
+            gap = sb.tile([P, K, P], F32, name=f"gap{h}")
             for k in range(K):
-                nc.vector.scalar_tensor_tensor(slope[:, k, :], back[:, 0, :], val_sb[:, k : k + 1], negc[:], ALU.subtract, ALU.mult)
-            t2.append(slope)
+                nc.scalar.activation(gap[:, k, :], ev_c[:, 0, :], ACT.Identity, bias=val_sb[:, k : k + 1], scale=-1.0)
+            gaps.append((ev_c, gap))
 
-        prods = []
-        terms = []
         for h in range(HALVES):
-            sums = group_sums(xx[h], h, "x")
-            means = sb.tile([P, 2, G], F32, name=f"means{h}")
-            nc.vector.scalar_tensor_tensor(means[:], sums[:], 8.0, coef[:, h, 0, :].unsqueeze(1).to_broadcast([P, 2, G]), ALU.mult, ALU.mult)
-            prod = sb.tile([P, 2, 2 * G, 2], F32, name=f"prod{h}")
-            nc.vector.tensor_tensor(
-                prod[:],
-                coef[:, h].rearrange("p (a q) g -> p a (q g)", a=2).unsqueeze(3).to_broadcast([P, 2, 2 * G, 2]),
-                means[:].rearrange("p q g -> p (q g)").unsqueeze(1).unsqueeze(3).to_broadcast([P, 2, 2 * G, 2]),
-                ALU.mult)
-            prods.append(prod)
+            for k in range(0, K, K_STEP):
+                ks = slice(k, k + K_STEP)
+                nc.vector.tensor_tensor(xv_x[h][:, 1, ks, :], ts_banks[h][:, ks, :], pv_p[h][:, 1, ks, :], ALU.mult)
+            times_val(xv_x[h])
+
+        ev = turned[:, :, 0, :, 0]
+        c = turned[:, :, 1, :, 0]
+        ev_rz = sb.tile([P, HALVES, G], F32, name="ev_rz", tag="d_codes0", align_bytes=MX_ALIGN)
+        c_a2 = sb.tile([P, HALVES, G], F32, name="c_a2")
+        nc.vector.tensor_tensor(ev_rz[:], coef[:, :, 0, :], ev, ALU.mult)
+        nc.vector.tensor_tensor(coef[:, :, 1:3, :], c.unsqueeze(2).to_broadcast([P, HALVES, 2, G]),
+                                ev_rz[:].unsqueeze(2).to_broadcast([P, HALVES, 2, G]), ALU.subtract)
+        nc.vector.tensor_tensor(c_a2[:], c, coef[:, :, 1, :], ALU.add)
+        nc.vector.scalar_tensor_tensor(coef[:, :, 3, :], c_a2[:], -1.0, ev, ALU.mult, ALU.mult)
+
+        terms = [sb.tile([P, 3, K, P], F32, name=f"terms{h}") for h in range(HALVES)]
         for h in range(HALVES):
-            three = sb.tile([P, 3, K, P], F32, name=f"terms{h}")
-            nc.vector.tensor_tensor(three[:, 2], xx[h][:, 1], t2[h][:], ALU.mult)
-            terms.append(three)
+            ev_c, gap = gaps[h]
+            slope = sb.tile([P, K, P], F32, name=f"slope{h}", tag=("d_codes1", "d_scales1")[h], align_bytes=MX_ALIGN)
+            nc.vector.scalar_tensor_tensor(slope[:], ev_c[:, 1, :].unsqueeze(1).to_broadcast([P, K, P]), -8.0, gap[:],
+                                           ALU.mult, ALU.mult)
+            nc.vector.tensor_tensor(terms[h][:, 2], xv_x[h][:, 1], slope[:], ALU.mult)
+
+        a_b = []
         for h in range(HALVES):
-            back = ps.tile([P, 2, P], F32, name=f"back_x{h}", tag=f"back{h}")
-            flat = prods[h][:].rearrange("p a c r -> p a (c r)")
-            turn_and_add([(back[:, a, :], flat[:, a, q * P : (q + 1) * P]) for a in range(2) for q in range(2)])
-            for a in range(2):
-                nc.vector.tensor_tensor(terms[h][:, a], back[:, a, :].unsqueeze(1).to_broadcast([P, K, P]), pp[h][:, a], ALU.mult)
+            bank = ps.tile([P, 2, P], F32, name=f"bank_x{h}", tag=f"sum{h}")
+            turn_and_add([(bank[:, n, :], xv_x[h][:, n, k, :]) for n in (1, 0) for k in range(K)])
+            xw_xz = sb.tile([P, 2, G], F32, name=f"xw_xz{h}")
+            nc.vector.tensor_reduce(xw_xz[:], bank[:].rearrange("i n (g e) -> i n g e", e=2), AX.X, ALU.add)
+            m = sb.tile([P, 2, G], F32, name=f"m{h}")
+            nc.vector.scalar_tensor_tensor(m[:], xw_xz[:], 8.0, coef[:, h, 0, :].unsqueeze(1).to_broadcast([P, 2, G]),
+                                           ALU.mult, ALU.mult)
+            parts = sb.tile([P, 2, 2 * G, 2], F32, name=f"parts{h}")
+            banks = []
+            for n in range(2):
+                nc.vector.tensor_tensor(parts[:, n], twice(coef[:, h, 2 * n : 2 * n + 2, :].rearrange("i q g -> i (q g)")),
+                                        twice(m[:].rearrange("i q g -> i (q g)")), ALU.mult)
+                flat = parts[:, n].rearrange("i x e -> i (x e)")
+                factor = ps.tile([P, P], F32, name=f"factor{h}{n}", tag=(f"back{h}", f"d_bank{h}")[n])
+                turn_and_add([(factor[:], flat[:, q * P : (q + 1) * P]) for q in range(2)])
+                banks.append(factor)
+            a_b.append(banks)
         for h in range(HALVES):
-            total = ps.tile([P, K, P], F32, name=f"total{h}", tag=f"s{h}")
-            turn_and_add([(total[:, k, :], terms[h][:, a, k, :]) for a in (2, 0, 1) for k in range(K)])
-            res = sb.tile([P, P, K], F32, name=f"res{h}")
-            nc.vector.tensor_tensor(res[:], total[:].rearrange("i k p -> i p k"), base_sb[h][:].rearrange("i (p k) -> i p k", k=K), ALU.add)
-            nc.sync.dma_start(out[h * P : (h + 1) * P, :], res[:].rearrange("i p k -> i (p k)"))
+            for n in range(2):
+                for k in range(0, K, K_STEP):
+                    ks = slice(k, k + K_STEP)
+                    nc.vector.tensor_tensor(terms[h][:, n, ks], a_b[h][n][:].unsqueeze(1).to_broadcast([P, K_STEP, P]),
+                                            pv_p[h][:, n, ks], ALU.mult)
+
+        for h in range(HALVES):
+            total = ps.tile([P, K, P], F32, name=f"total{h}", tag=f"a_bank{h}")
+            turn_and_add([(total[:, k, :], terms[h][:, n, k, :]) for n in (2, 0, 1) for k in range(K)])
+            width = P // 2 if h == HALVES - 1 else P
+            for r0 in range(0, P, width):
+                columns = slice(r0 * K, (r0 + width) * K)
+                result = sb.tile([P, width, K], F32, name=f"result{h}_{r0}")
+                nc.vector.tensor_tensor(result[:], total[:, :, r0 : r0 + width].rearrange("i k r -> i r k"),
+                                        base_sb[h][:, columns].rearrange("i (r k) -> i r k", k=K), ALU.add)
+                nc.sync.dma_start(out[h * P : (h + 1) * P, columns], result[:].rearrange("i r k -> i (r k)"))

from contextlib import ExitStack

import concourse.mybir as mybir
from concourse.masks import make_identity

D, T, U, I, J, G = 512, 1024, 1024, 256, 512, 64
FLOPS = 2 * 2 * D * I * J

F32 = mybir.dt.float32
BF16 = mybir.dt.bfloat16
I32 = mybir.dt.int32
U32 = mybir.dt.uint32
U16 = mybir.dt.uint16
U8 = mybir.dt.uint8
FP8X4 = mybir.dt.float8_e4m3fn_x4
FP4X4 = mybir.dt.float4_e2m1fn_x4
ALU = mybir.AluOpType
ACT = mybir.ActivationFunctionType
AX = mybir.AxisListType

P = 128
PACK = 4
HALVES = I // P
K = J // P
LIST_ROWS = 16
HALF_LIST = P // LIST_ROWS
K_STEP = 2
MX_ALIGN = 64


def tile_attend_hvexpectedvalue_kernel(tc, taba, dtab, tabb_words, tabb_scales, val, aim, base, offs, offs2, out):
    nc = tc.nc
    with ExitStack() as ctx:
        lists = ctx.enter_context(tc.tile_pool(name="lists", bufs=1))
        sb = ctx.enter_context(tc.tile_pool(name="sb", bufs=1))
        ps = ctx.enter_context(tc.psum_pool(name="ps", bufs=1))

        offs2_sb = lists.tile([P, J // LIST_ROWS], U16, name="offs2_sb")
        offs_sb = lists.tile([P, I // LIST_ROWS], U16, name="offs_sb")
        words = sb.tile([P, U], U16, name="words", align_bytes=MX_ALIGN)
        scales = sb.tile([P, U], U8, name="scales", align_bytes=MX_ALIGN)
        nc.gpsimd.memset(scales[:].bitcast(I32), 0)
        nc.sync.dma_start(offs2_sb[:], offs2)
        nc.sync.dma_start(words[:].bitcast(I32), tabb_words[0].bitcast(I32))
        for q in range(4):
            nc.sync.dma_start(scales[32 * q : 32 * q + 4, :].bitcast(I32), tabb_scales[0, 4 * q : 4 * q + 4, :].bitcast(I32))
        nc.sync.dma_start(offs_sb[:], offs)

        def load_planes(table, name):
            rows = table.rearrange("(r t) c -> r t c", t=PACK)
            planes = []
            for t in range(PACK):
                plane = sb.tile([P, T], F32, name=f"{name}{t}")
                nc.sync.dma_start(plane[:], rows[:, t, :])
                planes.append(plane)
            return planes

        a_planes = load_planes(taba, "a_plane")
        val_sb = sb.tile([P, K], F32, name="val_sb")
        nc.sync.dma_start(val_sb[:], val.rearrange("o (r k) -> (o r) k", k=K))
        d_planes = load_planes(dtab, "d_plane")
        aim_sb = sb.tile([P, HALVES, G], F32, name="aim_sb")
        nc.sync.dma_start(aim_sb[:], aim.rearrange("(h i) g -> i h g", i=P))
        base_sb = []
        for h in range(HALVES):
            rows = sb.tile([P, J], F32, name=f"base{h}")
            nc.sync.dma_start(rows[:], base[h * P : (h + 1) * P, :])
            base_sb.append(rows)

        ident = sb.tile([P, P], F32, name="ident")
        make_identity(nc, ident[:])

        got_words = sb.tile([P, J], U16, name="got_words", align_bytes=MX_ALIGN)
        got_scales = sb.tile([P, J], U8, name="got_scales", align_bytes=MX_ALIGN)
        b_words = sb.tile([P, K, P], U16, name="b_words", align_bytes=MX_ALIGN)
        b_scales = sb.tile([P, K, P], U8, name="b_scales", align_bytes=MX_ALIGN)
        nc.vector.tensor_copy(got_scales[:], scales[:].indirect(offs2_sb[:]))
        nc.vector.tensor_copy(got_words[:], words[:].indirect(offs2_sb[:]))
        nc.vector.tensor_copy(b_words[:], got_words[:].rearrange("p (r k) -> p k r", k=K))
        nc.vector.tensor_copy(b_scales[:], got_scales[:].rearrange("p (r k) -> p k r", k=K))

        def pieces(whole):
            if whole:
                return [(slice(0, I), slice(0, I // LIST_ROWS))]
            return [(slice(h * P, (h + 1) * P), slice(h * HALF_LIST, (h + 1) * HALF_LIST)) for h in range(HALVES)]

        def gather_on_vector(picked, plane, t, whole):
            for entries, columns in pieces(whole):
                nc.vector.tensor_copy(picked[:, entries, t], plane[:].indirect(offs_sb[:, columns]))

        def gather_on_scalar(picked, plane, t, whole):
            rounded = sb.tile([P, T], BF16, name=f"rounded{t}")
            nc.scalar.activation(rounded[:], plane[:], ACT.Copy)
            for entries, columns in pieces(whole):
                nc.scalar.activation(picked[:, entries, t], rounded[:].indirect(offs_sb[:, columns]), ACT.Copy)

        def scores(picked, name, h):
            codes = sb.tile([P, P], U32, name=f"{name}_codes{h}", align_bytes=MX_ALIGN)
            code_scales = sb.tile([P, P], U8, name=f"{name}_scales{h}", align_bytes=MX_ALIGN)
            nc.vector.quantize_mx(out=codes[:].bitcast(FP8X4), scales=code_scales[:],
                                  in_=picked[:, h * P : (h + 1) * P, :].rearrange("p i t -> p (i t)"))
            bank = ps.tile([P, K, P], F32, name=f"{name}_bank{h}")
            for k in range(K):
                nc.tensor.matmul_mx(out=bank[:, k, :], lhsT=b_words[:, k, :].bitcast(FP4X4), lhsT_scale=b_scales[:, k, :],
                                    rhs=codes[:].bitcast(FP8X4), rhs_scale=code_scales[:], start=True, stop=True)
            return bank

        def turn_and_add(steps):
            for n, (place, tile) in enumerate(steps):
                nc.tensor.matmul(place, tile, ident[:], start=(n == 0), stop=(n == len(steps) - 1), is_transpose=True)

        def times_val(pair):
            for k in range(K):
                nc.scalar.activation(pair[:, 0, k, :], pair[:, 1, k, :], ACT.Copy, scale=val_sb[:, k : k + 1])

        def group_sum(tiles, name, bank_tag, buffer_tag, align):
            bank = ps.tile([P, P], F32, name=f"bank_{name}", tag=bank_tag)
            turn_and_add([(bank[:], tiles[:, k, :]) for k in range(K)])
            total = sb.tile([P, G], F32, name=name, tag=buffer_tag, align_bytes=align)
            nc.vector.tensor_reduce(total[:], bank[:].rearrange("i (g e) -> i g e", e=2), AX.X, ALU.add)
            return total

        def twice(ap):
            return ap.unsqueeze(2).to_broadcast([P, ap.shape[1], 2])

        a_picked = sb.tile([P, I, PACK], BF16, name="a_picked", align_bytes=MX_ALIGN)
        d_picked = sb.tile([P, I, PACK], BF16, name="d_picked", align_bytes=MX_ALIGN)
        for t in (0, 1):
            gather_on_scalar(a_picked, a_planes[t], t, whole=(t == 0))
        for t in (2, 3):
            gather_on_vector(a_picked, a_planes[t], t, whole=(t == 2))
        s_banks = [scores(a_picked, "a", h) for h in range(HALVES)]
        pv_p = []
        for h in range(HALVES):
            pair = sb.tile([P, 2, K, P], F32, name=f"pv_p{h}")
            nc.scalar.activation(pair[:, 1], s_banks[h][:], ACT.Exp)
            pv_p.append(pair)
        for h in range(HALVES):
            times_val(pv_p[h])

        turned = sb.tile([P, HALVES, 2, G, 2], F32, name="turned")
        for t in range(PACK):
            gather_on_vector(d_picked, d_planes[t], t, whole=(t < PACK - 1))
        ts_banks = [scores(d_picked, "d", h) for h in range(HALVES)]

        coef = sb.tile([P, HALVES, 4, G], F32, name="coef", tag="d_plane3")
        xv_x = [sb.tile([P, 2, K, P], F32, name=f"xv_x{h}") for h in range(HALVES)]
        for h in range(HALVES):
            z = group_sum(pv_p[h][:, 1], f"z{h}", f"sum{h}", "d_plane2", None)
            nc.vector.reciprocal(coef[:, h, 0, :], z[:])
        gaps = []
        for h in range(HALVES):
            rz = coef[:, h, 0, :]
            buffer_tag, align = (("d_picked", MX_ALIGN), ("d_plane2", None))[h]
            w = group_sum(pv_p[h][:, 0], f"w{h}", f"back{h}", buffer_tag, align)
            nc.vector.tensor_tensor(turned[:, h, 0], twice(w[:]), twice(rz), ALU.mult)
            miss = sb.tile([P, G], F32, name=f"miss{h}")
            nc.vector.tensor_tensor(miss[:], aim_sb[:, h, :], turned[:, h, 0, :, 0], ALU.subtract)
            nc.vector.tensor_tensor(turned[:, h, 1], twice(miss[:]), twice(rz), ALU.mult)
            ev_c = ps.tile([P, 2, P], F32, name=f"ev_c{h}", tag=f"a_bank{h}")
            turn_and_add([(ev_c[:, n, :], turned[:, h, n].rearrange("i g e -> i (g e)")) for n in range(2)])
            gap = sb.tile([P, K, P], F32, name=f"gap{h}")
            for k in range(K):
                nc.scalar.activation(gap[:, k, :], ev_c[:, 0, :], ACT.Identity, bias=val_sb[:, k : k + 1], scale=-1.0)
            gaps.append((ev_c, gap))

        for h in range(HALVES):
            for k in range(0, K, K_STEP):
                ks = slice(k, k + K_STEP)
                nc.vector.tensor_tensor(xv_x[h][:, 1, ks, :], ts_banks[h][:, ks, :], pv_p[h][:, 1, ks, :], ALU.mult)
            times_val(xv_x[h])

        ev = turned[:, :, 0, :, 0]
        c = turned[:, :, 1, :, 0]
        ev_rz = sb.tile([P, HALVES, G], F32, name="ev_rz", tag="d_codes0", align_bytes=MX_ALIGN)
        c_a2 = sb.tile([P, HALVES, G], F32, name="c_a2")
        nc.vector.tensor_tensor(ev_rz[:], coef[:, :, 0, :], ev, ALU.mult)
        nc.vector.tensor_tensor(coef[:, :, 1:3, :], c.unsqueeze(2).to_broadcast([P, HALVES, 2, G]),
                                ev_rz[:].unsqueeze(2).to_broadcast([P, HALVES, 2, G]), ALU.subtract)
        nc.vector.tensor_tensor(c_a2[:], c, coef[:, :, 1, :], ALU.add)
        nc.vector.scalar_tensor_tensor(coef[:, :, 3, :], c_a2[:], -1.0, ev, ALU.mult, ALU.mult)

        terms = [sb.tile([P, 3, K, P], F32, name=f"terms{h}") for h in range(HALVES)]
        for h in range(HALVES):
            ev_c, gap = gaps[h]
            slope = sb.tile([P, K, P], F32, name=f"slope{h}", tag=("d_codes1", "d_scales1")[h], align_bytes=MX_ALIGN)
            nc.vector.scalar_tensor_tensor(slope[:], ev_c[:, 1, :].unsqueeze(1).to_broadcast([P, K, P]), -8.0, gap[:],
                                           ALU.mult, ALU.mult)
            nc.vector.tensor_tensor(terms[h][:, 2], xv_x[h][:, 1], slope[:], ALU.mult)

        a_b = []
        for h in range(HALVES):
            bank = ps.tile([P, 2, P], F32, name=f"bank_x{h}", tag=f"sum{h}")
            turn_and_add([(bank[:, n, :], xv_x[h][:, n, k, :]) for n in (1, 0) for k in range(K)])
            xw_xz = sb.tile([P, 2, G], F32, name=f"xw_xz{h}")
            nc.vector.tensor_reduce(xw_xz[:], bank[:].rearrange("i n (g e) -> i n g e", e=2), AX.X, ALU.add)
            m = sb.tile([P, 2, G], F32, name=f"m{h}")
            nc.vector.scalar_tensor_tensor(m[:], xw_xz[:], 8.0, coef[:, h, 0, :].unsqueeze(1).to_broadcast([P, 2, G]),
                                           ALU.mult, ALU.mult)
            parts = sb.tile([P, 2, 2 * G, 2], F32, name=f"parts{h}")
            banks = []
            for n in range(2):
                nc.vector.tensor_tensor(parts[:, n], twice(coef[:, h, 2 * n : 2 * n + 2, :].rearrange("i q g -> i (q g)")),
                                        twice(m[:].rearrange("i q g -> i (q g)")), ALU.mult)
                flat = parts[:, n].rearrange("i x e -> i (x e)")
                factor = ps.tile([P, P], F32, name=f"factor{h}{n}", tag=(f"back{h}", f"d_bank{h}")[n])
                turn_and_add([(factor[:], flat[:, q * P : (q + 1) * P]) for q in range(2)])
                banks.append(factor)
            a_b.append(banks)
        for h in range(HALVES):
            for n in range(2):
                for k in range(0, K, K_STEP):
                    ks = slice(k, k + K_STEP)
                    nc.vector.tensor_tensor(terms[h][:, n, ks], a_b[h][n][:].unsqueeze(1).to_broadcast([P, K_STEP, P]),
                                            pv_p[h][:, n, ks], ALU.mult)

        for h in range(HALVES):
            total = ps.tile([P, K, P], F32, name=f"total{h}", tag=f"a_bank{h}")
            turn_and_add([(total[:, k, :], terms[h][:, n, k, :]) for n in (2, 0, 1) for k in range(K)])
            width = P // 2 if h == HALVES - 1 else P
            for r0 in range(0, P, width):
                columns = slice(r0 * K, (r0 + width) * K)
                result = sb.tile([P, width, K], F32, name=f"result{h}_{r0}")
                nc.vector.tensor_tensor(result[:], total[:, :, r0 : r0 + width].rearrange("i k r -> i r k"),
                                        base_sb[h][:, columns].rearrange("i (r k) -> i r k", k=K), ALU.add)
                nc.sync.dma_start(out[h * P : (h + 1) * P, columns], result[:].rearrange("i r k -> i (r k)"))
